import numpy as np
import ml_dtypes


def mxq(x, axis, fmt="e4m3"):
    dtype, down = {"e4m3": (ml_dtypes.float8_e4m3fn, 7), "e5m2": (ml_dtypes.float8_e5m2, 14)}[fmt]
    v = np.moveaxis(np.asarray(x, np.float32).astype(ml_dtypes.bfloat16).astype(np.float64), axis, -1)
    blocks = v.reshape(v.shape[:-1] + (-1, 32))
    amax = np.abs(blocks).max(-1, keepdims=True)
    byte = np.maximum(np.where(amax > 0, np.frexp(amax)[1] - 1 + 127, 0) - down, 1)
    scale = np.exp2(byte - 127.0)
    codes = (blocks / scale).astype(np.float32).astype(dtype).astype(np.float64)
    return np.moveaxis((codes * scale).reshape(v.shape), -1, axis)


WIDE = False


def mx_kscale(k):
    if not WIDE:
        return np.ones(k)
    levels = np.array([30, -30])
    if k % 512:
        return np.exp2(np.random.permutation(np.resize(levels, k // 32))).repeat(32)
    a = np.empty((k // 512, 16))
    for p in range(k // 512):
        a[p, :8] = np.random.permutation(np.resize(levels, 8))
        for g in range(8):
            far = levels[np.abs(levels - a[p, g]) >= 10]
            a[p, g + 8] = far[np.random.randint(len(far))]
    return np.exp2(a.ravel()).repeat(32)


def f64(x):
    return np.asarray(x).astype(np.float64)


def striped(idx):
    return np.tile(np.asarray(idx).reshape(-1, 16).T, (8, 1)).astype(np.uint16)


def unstriped(offs):
    return offs[:16].T.reshape(-1).astype(np.int64)


E2M1 = np.array([0.0, 0.5, 1.0, 1.5, 2.0, 3.0, 4.0, 6.0, -0.0, -0.5, -1.0, -1.5, -2.0, -3.0, -4.0, -6.0])


def pack_weight(w, fmt):
    k, n = w.shape
    w = f64(np.asarray(w, np.float32).astype(ml_dtypes.bfloat16)).reshape(k // 32, 32, n)
    amax = np.abs(w).max(1)
    if fmt == "e4m3":
        byte = np.frexp(amax)[1] - 1 + 127 - 7
    else:
        mant, ex = np.frexp(amax / 6.0)
        byte = np.where(mant > 0.5, ex, ex - 1) + 127
    byte = np.clip(np.where(amax > 0, byte, 1), 1, 254)
    scaled = (w * np.exp2(127.0 - byte)[:, None, :]).reshape(k, n).astype(np.float32)
    by_word = np.ascontiguousarray(scaled.reshape(k // 512, 128, 4, n).transpose(0, 1, 3, 2))
    if fmt == "e4m3":
        words = by_word.astype(ml_dtypes.float8_e4m3fn).view(np.uint8)
    else:
        c = by_word.astype(ml_dtypes.float4_e2m1fn).view(np.uint8) & 0xF
        words = (c[..., 0::2] | (c[..., 1::2] << 4)).reshape(k // 512, 128, 2 * n)
    return np.ascontiguousarray(words), np.ascontiguousarray(byte.astype(np.uint8).reshape(k // 512, 16, n))


def unpack_weight(words, scales, fmt):
    g, _, n = scales.shape
    words = np.ascontiguousarray(words).reshape(g, 128, n, -1)
    if fmt == "e4m3":
        vals = words.view(ml_dtypes.float8_e4m3fn).astype(np.float64)
    else:
        nib = np.empty((g, 128, n, 4), np.uint8)
        nib[..., 0::2] = words & 0xF
        nib[..., 1::2] = words >> 4
        vals = E2M1[nib]
    vals = vals * np.repeat(np.exp2(scales.astype(np.float64) - 127.0), 8, axis=1)[..., None]
    return vals.transpose(0, 1, 3, 2).reshape(g * 512, n)


K, T, J, R, F, Z, C, O, N, L, E = 512, 1024, 256, 512, 512, 1024, 512, 128, 256, 512, 512


def setup_inputs():
    n = np.random.standard_normal
    idx = np.random.permutation(T)[:J]
    idx2 = np.random.permutation(Z)[:J]
    idx3 = np.random.permutation(C)[:J]
    idx4 = np.random.permutation(C)[:O]
    idx5 = np.random.permutation(J)[:O]
    idx6 = np.random.permutation(E)[:O]
    idx7 = np.random.permutation(E)[:O]
    ff = mx_kscale(F)
    fk = mx_kscale(K)
    fr = mx_kscale(R)
    fl = mx_kscale(L)
    xop = pack_weight(n((F, Z)) / ff[:, None], "e4m3")
    wp = pack_weight(n((K, R)) * 1 / np.sqrt(K) / fk[:, None] * fr, "e4m3")
    w2p = pack_weight(n((F, R)) * 1 / np.sqrt(F) * ff[:, None], "e2m1")
    wbp = pack_weight(n((R, N)) * 1 / np.sqrt(R) / fr[:, None], "e2m1")
    sxp = pack_weight(n((L, O)) / fl[:, None], "e4m3")
    wsp = pack_weight(n((L, N)) * 1 / np.sqrt(L) * fl[:, None], "e4m3")
    return {
        "xo_words": xop[0],
        "xo_scales": xop[1],
        "cq": (np.random.randint(-7, 8, (K, T)).astype(np.float64)).astype(np.float32),
        "gs": (np.random.uniform(0.1, 0.4, (K, 1)) * fk[:, None]).astype(np.float32),
        "w_words": wp[0],
        "w_scales": wp[1],
        "w2_words": w2p[0],
        "w2_scales": w2p[1],
        "wb_words": wbp[0],
        "wb_scales": wbp[1],
        "sx_words": sxp[0],
        "sx_scales": sxp[1],
        "ws_words": wsp[0],
        "ws_scales": wsp[1],
        "offs": striped(idx),
        "offs2": striped(idx2),
        "offs3": striped(idx3),
        "offs4": striped(idx4),
        "offs5": striped(idx5),
        "offs6": striped(idx6),
        "offs7": striped(idx7),
    }


def reference(xo_words, xo_scales, cq, gs, w_words, w_scales, w2_words, w2_scales, wb_words, wb_scales, sx_words, sx_scales, ws_words, ws_scales, offs, offs2, offs3, offs4, offs5, offs6, offs7):
    idx = unstriped(offs)
    idx2 = unstriped(offs2)
    idx3 = unstriped(offs3)
    idx4 = unstriped(offs4)
    idx5 = unstriped(offs5)
    idx6 = unstriped(offs6)
    idx7 = unstriped(offs7)
    xou = unpack_weight(xo_words, xo_scales, "e4m3")
    wu = unpack_weight(w_words, w_scales, "e4m3")
    w2u = unpack_weight(w2_words, w2_scales, "e2m1")
    wbu = unpack_weight(wb_words, wb_scales, "e2m1")
    sxu = unpack_weight(sx_words, sx_scales, "e4m3")
    wsu = unpack_weight(ws_words, ws_scales, "e4m3")
    x1 = f64(cq)[:, idx] * f64(gs)
    x1q = mxq(x1, 0, "e4m3")
    a = wu.T @ x1q
    xoidx2g = xou[:, idx2]
    b = w2u.T @ xoidx2g
    lb = b[:, 0:1]
    la = a[:, 0:1]
    pw = np.zeros((R, C))
    pw[:, idx3] = a
    hid = np.maximum(pw[:, idx4] * lb, b[:, idx5] * la)
    hidq = mxq(hid, 0, "e5m2")
    p = wbu.T @ hidq + wsu.T @ sxu
    pa = np.zeros((N, E))
    pa[:, idx6] = p
    pb = np.zeros((N, E))
    pb[:, idx7] = p
    y = pa + pb
    return y

@@ -1,0 +1,209 @@
+from contextlib import ExitStack
+
+import concourse.mybir as mybir
+
+F32 = mybir.dt.float32
+BF16 = mybir.dt.bfloat16
+I32 = mybir.dt.int32
+U32 = mybir.dt.uint32
+U16 = mybir.dt.uint16
+U8 = mybir.dt.uint8
+E4M3 = mybir.dt.float8_e4m3fn_x4
+E5M2 = mybir.dt.float8_e5m2_x4
+E2M1 = mybir.dt.float4_e2m1fn_x4
+COPY = mybir.ActivationFunctionType.Copy
+
+P = 128
+PACK = 4
+QUADS = 4
+K, T, J, R, Z, C, O, N, E = 512, 1024, 256, 512, 1024, 512, 128, 256, 512
+
+FLOPS = 2 * K * R * J * 2 + 2 * R * N * O * 2
+
+
+def tile_list_leadboard_codednote_further_pagetwice_kernel(
+    tc, xo_words, xo_scales, cq, gs, w_words, w_scales, w2_words, w2_scales, wb_words, wb_scales,
+    sx_words, sx_scales, ws_words, ws_scales, offs, offs2, offs3, offs4, offs5, offs6, offs7, out,
+):
+    nc = tc.nc
+
+    def words8(ap):
+        return ap[0].rearrange("p n t -> p (n t)").bitcast(I32)
+
+    def words4(ap):
+        return ap[0].bitcast(I32)
+
+    def scale_rows(ap):
+        return ap[0].bitcast(I32).rearrange("(q r) n -> r q n", q=QUADS)
+
+    with ExitStack() as ctx:
+        sb = ctx.enter_context(tc.tile_pool(name="sb", bufs=1))
+        ps = ctx.enter_context(tc.psum_pool(name="ps", bufs=1))
+
+        def tile(name, shape, dtype, tag=None):
+            return sb.tile(shape, dtype, name=name, tag=tag or name, align_bytes=64)
+
+        o1 = tile("o1", [P, J // 16], U16)
+        o2 = tile("o2", [P, J // 16], U16)
+        o3 = tile("o3", [P, J // 16], U16)
+        o4 = tile("o4", [P, O // 16], U16)
+        o5 = tile("o5", [P, O // 16], U16)
+        o6 = tile("o6", [P, O // 16], U16)
+        o7 = tile("o7", [P, O // 16], U16)
+        gs_sb = tile("gs_sb", [P, PACK], F32)
+        cq_sb = [tile("cq%d" % t, [P, T], F32) for t in range(PACK)]
+        xo_w = tile("xo_w", [P, Z], I32)
+        w_raw = tile("w_raw", [P, R], I32)
+        w2_raw = tile("w2_raw", [P, R // 2], I32)
+        wb_w = tile("wb_w", [P, 2 * N], U8)
+        ws_w = tile("ws_w", [P, N], I32)
+        sx_w = tile("sx_w", [P, O], I32)
+        stage_x = tile("stage_x", [4, QUADS, Z // 4], I32)
+        stage_a = tile("stage_a", [P, QUADS, R // 4], I32)
+        stage_b = tile("stage_b", [32, QUADS, N // 4], I32)
+        plane_x = tile("plane_x", [P, Z], U8)
+        raw_a = tile("raw_a", [P, R], U8)
+        plane_a = tile("plane_a", [P, R], U8)
+        plane_b = tile("plane_b", [P, N], U8)
+        pw = [tile("pw%d" % t, [P, C], F32) for t in range(PACK)]
+        pa = [tile("pa%d" % h, [P, E], F32) for h in range(2)]
+        pb = [tile("pb%d" % h, [P, E], F32) for h in range(2)]
+
+        nc.vector.memset(stage_a[64:96], 0)
+        nc.vector.memset(stage_b[:], 0)
+        nc.vector.memset(plane_x[:].bitcast(I32), 0)
+
+        cq_rows = cq.rearrange("(p t) n -> p t n", t=PACK)
+        nc.sync.dma_start(o1[:], offs)
+        nc.sync.dma_start(cq_sb[0][:], cq_rows[:, 0, :])
+        nc.sync.dma_start(gs_sb[:], gs.rearrange("(p t) o -> p (t o)", t=PACK))
+        nc.sync.dma_start(stage_x[:], scale_rows(xo_scales))
+        nc.sync.dma_start(o2[:], offs2)
+        nc.sync.dma_start(stage_a[68:72], scale_rows(w_scales))
+        nc.sync.dma_start(stage_a[64:68], scale_rows(w2_scales))
+        nc.sync.dma_start(cq_sb[1][:], cq_rows[:, 1, :])
+        nc.sync.dma_start(cq_sb[2][:], cq_rows[:, 2, :])
+        nc.sync.dma_start(stage_b[0:4], scale_rows(wb_scales))
+        nc.sync.dma_start(stage_b[4:8, :, 0 : O // 4], scale_rows(sx_scales))
+        nc.sync.dma_start(stage_b[8:12], scale_rows(ws_scales))
+        nc.sync.dma_start(cq_sb[3][:], cq_rows[:, 3, :])
+        nc.sync.dma_start(w_raw[:], words8(w_words))
+        nc.sync.dma_start(w2_raw[:], words4(w2_words))
+        nc.sync.dma_start(xo_w[:], words8(xo_words))
+        nc.sync.dma_start(o3[:], offs3)
+        nc.sync.dma_start(o5[:], offs5)
+        nc.sync.dma_start(o4[:], offs4)
+        nc.sync.dma_start(sx_w[:], words8(sx_words))
+        nc.sync.dma_start(ws_w[:], words8(ws_words))
+        nc.sync.dma_start(wb_w[:].bitcast(I32), words4(wb_words))
+        nc.sync.dma_start(o6[:], offs6)
+        nc.sync.dma_start(o7[:], offs7)
+
+        for page in pw + pa + pb:
+            nc.vector.memset(page[:], 0.0)
+
+        for q in range(QUADS):
+            nc.vector.tensor_copy(plane_x[:].bitcast(I32)[32 * q : 32 * q + 4, :], stage_x[:, q, :])
+        xg_s = tile("xg_s", [P, J], U8)
+        nc.vector.tensor_copy(xg_s[:], plane_x[:].indirect(o2[:]))
+        for q in range(QUADS):
+            nc.vector.tensor_copy(raw_a[:].bitcast(I32)[32 * q : 32 * q + 32, :], stage_a[64:96, q, :])
+        nc.vector.tensor_copy(
+            plane_a[:].rearrange("p (t m) -> p t m", t=PACK), raw_a[:].rearrange("p (m t) -> p t m", t=PACK)
+        )
+        for q in range(QUADS):
+            nc.vector.tensor_copy(plane_b[:].bitcast(I32)[32 * q : 32 * q + 32, :], stage_b[:, q, :])
+
+        x1_pairs = [tile("x1_pair%d" % u, [P, 2, J], BF16) for u in range(2)]
+        x1_in = tile("x1_in", [P, J, PACK], BF16)
+        for t in range(PACK):
+            nc.scalar.activation(
+                x1_pairs[t // 2][:, t % 2, :], cq_sb[t][:].indirect(o1[:]), COPY, scale=gs_sb[:, t : t + 1]
+            )
+            if t % 2 == 1:
+                nc.vector.tensor_copy(x1_in[:, :, t - 1 : t + 1], x1_pairs[t // 2][:].rearrange("p t j -> p j t"))
+        x1_w = tile("x1_w", [P, J], U32)
+        x1_s = tile("x1_s", [P, J], U8)
+        nc.vector.quantize_mx(out=x1_w[:].bitcast(E4M3), scales=x1_s[:], in_=x1_in[:].rearrange("p j t -> p (j t)"))
+
+        w_w = tile("w_w", [P, R], U32)
+        nc.scalar.copy(
+            w_w[:].rearrange("p (t m) -> p t m", t=PACK),
+            w_raw[:].bitcast(U32).rearrange("p (m t) -> p t m", t=PACK),
+        )
+        w2_w = tile("w2_w", [P, 2 * R], U8)
+        nc.scalar.copy(
+            w2_w[:].bitcast(U16).rearrange("p (t m) -> p t m", t=PACK),
+            w2_raw[:].bitcast(U16).rearrange("p (m t) -> p t m", t=PACK),
+        )
+        xg_w = tile("xg_w", [P, J], U32)
+        nc.vector.tensor_copy(xg_w[:], xo_w[:].bitcast(U32).indirect(o2[:]))
+
+        a_ps = [ps.tile([P, J], F32, name="a_ps%d" % t) for t in range(PACK)]
+        b_ps = [ps.tile([P, 2, J], F32, name="b_ps%d" % u) for u in range(2)]
+        p_ps = [ps.tile([P, O], F32, name="p_ps%d" % h) for h in range(2)]
+        for t in range(PACK):
+            cols = slice(P * t, P * (t + 1))
+            nc.tensor.matmul_mx(
+                out=a_ps[t][:], lhsT=w_w[:, cols].bitcast(E4M3), lhsT_scale=plane_a[4:P, cols],
+                rhs=x1_w[:].bitcast(E4M3), rhs_scale=x1_s[:], start=True, stop=True,
+            )
+        for t in range(PACK):
+            cols = slice(P * t, P * (t + 1))
+            nc.tensor.matmul_mx(
+                out=b_ps[t // 2][:, t % 2, :], lhsT=w2_w[:, 2 * P * t : 2 * P * (t + 1)].bitcast(E2M1),
+                lhsT_scale=plane_a[:, cols], rhs=xg_w[:].bitcast(E4M3), rhs_scale=xg_s[:], start=True, stop=True,
+            )
+        for h in range(2):
+            cols = slice(P * h, P * (h + 1))
+            nc.tensor.matmul_mx(
+                out=p_ps[h][:], lhsT=ws_w[:, cols].bitcast(E4M3), lhsT_scale=plane_b[8:P, cols],
+                rhs=sx_w[:].bitcast(E4M3), rhs_scale=plane_b[4:P, 0:O], start=True, stop=False,
+            )
+
+        a_sb = [tile("a_sb%d" % t, [P, J], F32, tag="xo_w" if t == 1 else None) for t in range(PACK)]
+        b_sb = [tile("b_sb%d" % t, [P, J], F32) for t in range(PACK)]
+        from_pw = tile("from_pw", [P, PACK, O], F32)
+        from_b = tile("from_b", [P, PACK, O], F32)
+
+        def gather_pw(t):
+            nc.scalar.activation(from_pw[:, t, :], pw[t][:].indirect(o4[:]), COPY, scale=b_sb[t][:, 0:1])
+
+        nc.scalar.copy(a_sb[0][:], a_ps[0][:])
+        nc.scalar.activation(pw[0][:].indirect(o3[:]), a_sb[0][:], COPY)
+        for t in range(1, PACK):
+            nc.vector.tensor_copy(a_sb[t][:], a_ps[t][:])
+        for t in range(1, PACK):
+            nc.vector.tensor_copy(pw[t][:].indirect(o3[:]), a_sb[t][:])
+        for t in range(PACK):
+            nc.scalar.copy(b_sb[t][:], b_ps[t // 2][:, t % 2, :])
+        for t in range(PACK):
+            nc.scalar.activation(from_b[:, t, :], b_sb[t][:].indirect(o5[:]), COPY, scale=a_sb[t][:, 0:1])
+        for t in range(PACK):
+            gather_pw(t)
+
+        hid_in = tile("hid_in", [P, O, PACK], BF16)
+        nc.vector.tensor_max(
+            hid_in[:].rearrange("p (c i) t -> p c t i", i=4),
+            from_pw[:].rearrange("p t (c i) -> p c t i", i=4),
+            from_b[:].rearrange("p t (c i) -> p c t i", i=4),
+        )
+        hid_w = tile("hid_w", [P, O], U32)
+        hid_s = tile("hid_s", [P, O], U8)
+        nc.vector.quantize_mx(out=hid_w[:].bitcast(E5M2), scales=hid_s[:], in_=hid_in[:].rearrange("p o t -> p (o t)"))
+        for h in range(2):
+            nc.tensor.matmul_mx(
+                out=p_ps[h][:], lhsT=wb_w[:, 2 * P * h : 2 * P * (h + 1)].bitcast(E2M1),
+                lhsT_scale=plane_b[:, P * h : P * (h + 1)], rhs=hid_w[:].bitcast(E5M2), rhs_scale=hid_s[:],
+                start=False, stop=True,
+            )
+
+        p_sb = [tile("p_sb%d" % h, [P, O], F32) for h in range(2)]
+        y = [tile("y%d" % h, [P, E], F32) for h in range(2)]
+        nc.vector.tensor_copy(p_sb[0][:], p_ps[0][:])
+        nc.scalar.copy(p_sb[1][:], p_ps[1][:])
+        for h in range(2):
+            nc.vector.tensor_copy(pa[h][:].indirect(o6[:]), p_sb[h][:])
+            nc.scalar.activation(pb[h][:].indirect(o7[:]), p_sb[h][:], COPY)
+            nc.vector.tensor_add(y[h][:], pa[h][:], pb[h][:])
+            nc.sync.dma_start(out[P * h : P * (h + 1), :], y[h][:])

@@ -58,61 +58,68 @@ def tile_list_leadboard_codednote_further_pagetwice_kernel(
         wb_w = tile("wb_w", [P, 2 * N], U8)
         ws_w = tile("ws_w", [P, N], I32)
         sx_w = tile("sx_w", [P, O], I32)
-        stage_x = tile("stage_x", [4, QUADS, Z // 4], I32)
-        stage_a = tile("stage_a", [P, QUADS, R // 4], I32)
-        stage_b = tile("stage_b", [32, QUADS, N // 4], I32)
-        plane_x = tile("plane_x", [P, Z], U8)
-        raw_a = tile("raw_a", [P, R], U8)
-        plane_a = tile("plane_a", [P, R], U8)
+        stage_x = tile("stage_x", [16, Z // 4], I32)
+        stage_a = tile("stage_a", [8, QUADS, R // 4], I32)
         plane_b = tile("plane_b", [P, N], U8)
+        plane_x = tile("plane_x", [P, Z], U8)
+        raw_a = tile("raw_a", [P, 2, R // 4], I32)
+        plane_a = tile("plane_a", [P, R], U8)
+        xg_s = tile("xg_s", [P, J], U8)
         pw = [tile("pw%d" % t, [P, C], F32) for t in range(PACK)]
         pa = [tile("pa%d" % h, [P, E], F32) for h in range(2)]
         pb = [tile("pb%d" % h, [P, E], F32) for h in range(2)]
 
-        nc.vector.memset(stage_a[64:96], 0)
-        nc.vector.memset(stage_b[:], 0)
         nc.vector.memset(plane_x[:].bitcast(I32), 0)
+        nc.vector.memset(raw_a[:], 0)
+        nc.vector.memset(xg_s[:].bitcast(I32), 0)
+        nc.vector.memset(plane_b[:].bitcast(I32), 0)
 
         cq_rows = cq.rearrange("(p t) n -> p t n", t=PACK)
-        nc.sync.dma_start(o1[:], offs)
+        nc.sync.dma_start(stage_a[4:8], scale_rows(w_scales))
+        nc.sync.dma_start(stage_a[0:4], scale_rows(w2_scales))
+        nc.sync.dma_start(stage_x[:], xo_scales[0].bitcast(I32))
         nc.sync.dma_start(cq_sb[0][:], cq_rows[:, 0, :])
+        nc.sync.dma_start(o1[:], offs)
         nc.sync.dma_start(gs_sb[:], gs.rearrange("(p t) o -> p (t o)", t=PACK))
-        nc.sync.dma_start(stage_x[:], scale_rows(xo_scales))
         nc.sync.dma_start(o2[:], offs2)
-        nc.sync.dma_start(stage_a[68:72], scale_rows(w_scales))
-        nc.sync.dma_start(stage_a[64:68], scale_rows(w2_scales))
-        nc.sync.dma_start(cq_sb[1][:], cq_rows[:, 1, :])
-        nc.sync.dma_start(cq_sb[2][:], cq_rows[:, 2, :])
-        nc.sync.dma_start(stage_b[0:4], scale_rows(wb_scales))
-        nc.sync.dma_start(stage_b[4:8, :, 0 : O // 4], scale_rows(sx_scales))
-        nc.sync.dma_start(stage_b[8:12], scale_rows(ws_scales))
-        nc.sync.dma_start(cq_sb[3][:], cq_rows[:, 3, :])
+        for t in range(1, PACK):
+            nc.sync.dma_start(cq_sb[t][:], cq_rows[:, t, :])
         nc.sync.dma_start(w_raw[:], words8(w_words))
         nc.sync.dma_start(w2_raw[:], words4(w2_words))
         nc.sync.dma_start(xo_w[:], words8(xo_words))
+
+        nc.vector.tensor_copy(plane_x[:].bitcast(I32)[0:16, :], stage_x[:])
+        xg_rows = tile("xg_rows", [P, J], U8)
+        nc.vector.tensor_copy(xg_rows[:], plane_x[:].indirect(o2[:]))
+        nc.vector.tensor_copy(xg_s[:].bitcast(I32)[0:4, :], xg_rows[:].bitcast(I32)[0:4, :])
+        for q in range(1, QUADS):
+            nc.sync.dma_start(xg_s[:].bitcast(I32)[32 * q : 32 * q + 4, :], xg_rows[:].bitcast(I32)[4 * q : 4 * q + 4, :])
+
         nc.sync.dma_start(o3[:], offs3)
         nc.sync.dma_start(o5[:], offs5)
         nc.sync.dma_start(o4[:], offs4)
+        nc.sync.dma_start(o7[:], offs7)
+        nc.sync.dma_start(o6[:], offs6)
         nc.sync.dma_start(sx_w[:], words8(sx_words))
         nc.sync.dma_start(ws_w[:], words8(ws_words))
         nc.sync.dma_start(wb_w[:].bitcast(I32), words4(wb_words))
-        nc.sync.dma_start(o6[:], offs6)
-        nc.sync.dma_start(o7[:], offs7)
+        for first, scales, width in ((4, sx_scales, O), (8, ws_scales, N), (0, wb_scales, N)):
+            for q in range(QUADS):
+                nc.sync.dma_start(
+                    plane_b[32 * q + first : 32 * q + first + 4, 0:width].bitcast(I32),
+                    scales[0].bitcast(I32)[4 * q : 4 * q + 4, :],
+                )
 
-        for page in pw + pa + pb:
-            nc.vector.memset(page[:], 0.0)
 
-        for q in range(QUADS):
-            nc.vector.tensor_copy(plane_x[:].bitcast(I32)[32 * q : 32 * q + 4, :], stage_x[:, q, :])
-        xg_s = tile("xg_s", [P, J], U8)
-        nc.vector.tensor_copy(xg_s[:], plane_x[:].indirect(o2[:]))
-        for q in range(QUADS):
-            nc.vector.tensor_copy(raw_a[:].bitcast(I32)[32 * q : 32 * q + 32, :], stage_a[64:96, q, :])
+        for q in (2, 3, 0, 1):
+            nc.vector.tensor_copy(raw_a[32 * (q % 2) : 32 * (q % 2) + 8, q // 2, :], stage_a[:, q, :])
+        nc.vector.tensor_copy(raw_a[64:P, 0, :], raw_a[0:64, 1, :])
         nc.vector.tensor_copy(
-            plane_a[:].rearrange("p (t m) -> p t m", t=PACK), raw_a[:].rearrange("p (m t) -> p t m", t=PACK)
+            plane_a[:].rearrange("p (t m) -> p m t", t=PACK),
+            raw_a[:, 0, :].bitcast(U8).rearrange("p (m t) -> p m t", t=PACK),
         )
-        for q in range(QUADS):
-            nc.vector.tensor_copy(plane_b[:].bitcast(I32)[32 * q : 32 * q + 32, :], stage_b[:, q, :])
+        for page in pw + pa + pb:
+            nc.vector.memset(page[:].bitcast(I32), 0)
 
         x1_pairs = [tile("x1_pair%d" % u, [P, 2, J], BF16) for u in range(2)]
         x1_in = tile("x1_in", [P, J, PACK], BF16)
@@ -128,24 +135,26 @@ def tile_list_leadboard_codednote_further_pagetwice_kernel(
 
         w_w = tile("w_w", [P, R], U32)
         nc.scalar.copy(
-            w_w[:].rearrange("p (t m) -> p t m", t=PACK),
-            w_raw[:].bitcast(U32).rearrange("p (m t) -> p t m", t=PACK),
+            w_w[:].rearrange("p (t m) -> p m t", t=PACK),
+            w_raw[:].bitcast(U32).rearrange("p (m t) -> p m t", t=PACK),
         )
         w2_w = tile("w2_w", [P, 2 * R], U8)
         nc.scalar.copy(
-            w2_w[:].bitcast(U16).rearrange("p (t m) -> p t m", t=PACK),
-            w2_raw[:].bitcast(U16).rearrange("p (m t) -> p t m", t=PACK),
+            w2_w[:].bitcast(U16).rearrange("p (t m) -> p m t", t=PACK),
+            w2_raw[:].bitcast(U16).rearrange("p (m t) -> p m t", t=PACK),
         )
         xg_w = tile("xg_w", [P, J], U32)
         nc.vector.tensor_copy(xg_w[:], xo_w[:].bitcast(U32).indirect(o2[:]))
 
-        a_ps = [ps.tile([P, J], F32, name="a_ps%d" % t) for t in range(PACK)]
+        a_lone = [ps.tile([P, J], F32, name="a_ps%d" % t) for t in range(2)]
+        a_pair = ps.tile([P, 2, J], F32, name="a_pair")
+        a_ps = [a_lone[0][:], a_lone[1][:], a_pair[:, 0, :], a_pair[:, 1, :]]
         b_ps = [ps.tile([P, 2, J], F32, name="b_ps%d" % u) for u in range(2)]
         p_ps = [ps.tile([P, O], F32, name="p_ps%d" % h) for h in range(2)]
         for t in range(PACK):
             cols = slice(P * t, P * (t + 1))
             nc.tensor.matmul_mx(
-                out=a_ps[t][:], lhsT=w_w[:, cols].bitcast(E4M3), lhsT_scale=plane_a[4:P, cols],
+                out=a_ps[t], lhsT=w_w[:, cols].bitcast(E4M3), lhsT_scale=plane_a[4:P, cols],
                 rhs=x1_w[:].bitcast(E4M3), rhs_scale=x1_s[:], start=True, stop=True,
             )
         for t in range(PACK):
@@ -154,6 +163,30 @@ def tile_list_leadboard_codednote_further_pagetwice_kernel(
                 out=b_ps[t // 2][:, t % 2, :], lhsT=w2_w[:, 2 * P * t : 2 * P * (t + 1)].bitcast(E2M1),
                 lhsT_scale=plane_a[:, cols], rhs=xg_w[:].bitcast(E4M3), rhs_scale=xg_s[:], start=True, stop=True,
             )
+
+        a_first = tile("a_first", [P, J], F32, tag="w2_raw")
+        a_rest = tile("a_rest", [P, PACK - 1, J], F32, tag="xo_w")
+        a_sb = [a_first[:]] + [a_rest[:, t, :] for t in range(PACK - 1)]
+        b_sb = [tile("b_sb%d" % t, [P, J], F32) for t in range(PACK)]
+        from_pw = [tile("from_pw%d" % u, [P, 2, O], F32) for u in range(2)]
+        from_b = [tile("from_b%d" % u, [P, 2, O], F32) for u in range(2)]
+
+        def gather_pw(t):
+            nc.scalar.activation(from_pw[t // 2][:, t % 2, :], pw[t][:].indirect(o4[:]), COPY, scale=b_sb[t][:, 0:1])
+
+        nc.scalar.copy(a_sb[0], a_ps[0])
+        nc.scalar.activation(pw[0][:].indirect(o3[:]), a_sb[0], COPY)
+        nc.vector.tensor_copy(a_sb[1], a_ps[1])
+        nc.vector.tensor_copy(a_rest[:, 1:3, :], a_pair[:])
+        for t in range(1, PACK):
+            nc.vector.tensor_copy(pw[t][:].indirect(o3[:]), a_sb[t])
+        for t in range(PACK):
+            nc.scalar.copy(b_sb[t][:], b_ps[t // 2][:, t % 2, :])
+        for t in range(PACK):
+            nc.scalar.activation(from_b[t // 2][:, t % 2, :], b_sb[t][:].indirect(o5[:]), COPY, scale=a_sb[t][:, 0:1])
+        for t in range(PACK):
+            gather_pw(t)
+
         for h in range(2):
             cols = slice(P * h, P * (h + 1))
             nc.tensor.matmul_mx(
@@ -161,33 +194,13 @@ def tile_list_leadboard_codednote_further_pagetwice_kernel(
                 rhs=sx_w[:].bitcast(E4M3), rhs_scale=plane_b[4:P, 0:O], start=True, stop=False,
             )
 
-        a_sb = [tile("a_sb%d" % t, [P, J], F32, tag="xo_w" if t == 1 else None) for t in range(PACK)]
-        b_sb = [tile("b_sb%d" % t, [P, J], F32) for t in range(PACK)]
-        from_pw = tile("from_pw", [P, PACK, O], F32)
-        from_b = tile("from_b", [P, PACK, O], F32)
-
-        def gather_pw(t):
-            nc.scalar.activation(from_pw[:, t, :], pw[t][:].indirect(o4[:]), COPY, scale=b_sb[t][:, 0:1])
-
-        nc.scalar.copy(a_sb[0][:], a_ps[0][:])
-        nc.scalar.activation(pw[0][:].indirect(o3[:]), a_sb[0][:], COPY)
-        for t in range(1, PACK):
-            nc.vector.tensor_copy(a_sb[t][:], a_ps[t][:])
-        for t in range(1, PACK):
-            nc.vector.tensor_copy(pw[t][:].indirect(o3[:]), a_sb[t][:])
-        for t in range(PACK):
-            nc.scalar.copy(b_sb[t][:], b_ps[t // 2][:, t % 2, :])
-        for t in range(PACK):
-            nc.scalar.activation(from_b[:, t, :], b_sb[t][:].indirect(o5[:]), COPY, scale=a_sb[t][:, 0:1])
-        for t in range(PACK):
-            gather_pw(t)
-
-        hid_in = tile("hid_in", [P, O, PACK], BF16)
-        nc.vector.tensor_max(
-            hid_in[:].rearrange("p (c i) t -> p c t i", i=4),
-            from_pw[:].rearrange("p t (c i) -> p c t i", i=4),
-            from_b[:].rearrange("p t (c i) -> p c t i", i=4),
-        )
+        hid_in = tile("hid_in", [P, O, PACK], BF16, tag="xo_w")
+        for u in range(2):
+            nc.vector.tensor_max(
+                hid_in[:, :, 2 * u : 2 * u + 2].rearrange("p (c i) t -> p c t i", i=4),
+                from_pw[u][:].rearrange("p t (c i) -> p c t i", i=4),
+                from_b[u][:].rearrange("p t (c i) -> p c t i", i=4),
+            )
         hid_w = tile("hid_w", [P, O], U32)
         hid_s = tile("hid_s", [P, O], U8)
         nc.vector.quantize_mx(out=hid_w[:].bitcast(E5M2), scales=hid_s[:], in_=hid_in[:].rearrange("p o t -> p (o t)"))
@@ -200,10 +213,17 @@ def tile_list_leadboard_codednote_further_pagetwice_kernel(
 
         p_sb = [tile("p_sb%d" % h, [P, O], F32) for h in range(2)]
         y = [tile("y%d" % h, [P, E], F32) for h in range(2)]
-        nc.vector.tensor_copy(p_sb[0][:], p_ps[0][:])
-        nc.scalar.copy(p_sb[1][:], p_ps[1][:])
+        nc.scalar.copy(p_sb[0][:], p_ps[0][:])
+        nc.vector.tensor_copy(p_sb[1][:], p_ps[1][:])
+        half = O // 2
+        nc.scalar.activation(pb[0][:].indirect(o7[:]), p_sb[0][:], COPY)
+        nc.vector.tensor_copy(pa[1][:].indirect(o6[:, 0 : half // 16]), p_sb[1][:, 0:half])
+        nc.vector.tensor_copy(pa[0][:].indirect(o6[:]), p_sb[0][:])
+        nc.scalar.activation(pb[1][:].indirect(o7[:]), p_sb[1][:], COPY)
+        nc.scalar.activation(pa[1][:].indirect(o6[:, half // 16 : O // 16]), p_sb[1][:, half:O], COPY)
         for h in range(2):
-            nc.vector.tensor_copy(pa[h][:].indirect(o6[:]), p_sb[h][:])
-            nc.scalar.activation(pb[h][:].indirect(o7[:]), p_sb[h][:], COPY)
-            nc.vector.tensor_add(y[h][:], pa[h][:], pb[h][:])
-            nc.sync.dma_start(out[P * h : P * (h + 1), :], y[h][:])
+            pieces = 1 + h
+            for piece in range(pieces):
+                cols = slice(E // pieces * piece, E // pieces * (piece + 1))
+                nc.vector.tensor_add(y[h][:, cols], pa[h][:, cols], pb[h][:, cols])
+                nc.sync.dma_start(out[P * h : P * (h + 1), cols], y[h][:, cols])

from contextlib import ExitStack

import concourse.mybir as mybir

F32 = mybir.dt.float32
BF16 = mybir.dt.bfloat16
I32 = mybir.dt.int32
U32 = mybir.dt.uint32
U16 = mybir.dt.uint16
U8 = mybir.dt.uint8
E4M3 = mybir.dt.float8_e4m3fn_x4
E5M2 = mybir.dt.float8_e5m2_x4
E2M1 = mybir.dt.float4_e2m1fn_x4
COPY = mybir.ActivationFunctionType.Copy

P = 128
PACK = 4
QUADS = 4
K, T, J, R, Z, C, O, N, E = 512, 1024, 256, 512, 1024, 512, 128, 256, 512

FLOPS = 2 * K * R * J * 2 + 2 * R * N * O * 2


def tile_list_leadboard_codednote_further_pagetwice_kernel(
    tc, xo_words, xo_scales, cq, gs, w_words, w_scales, w2_words, w2_scales, wb_words, wb_scales,
    sx_words, sx_scales, ws_words, ws_scales, offs, offs2, offs3, offs4, offs5, offs6, offs7, out,
):
    nc = tc.nc

    def words8(ap):
        return ap[0].rearrange("p n t -> p (n t)").bitcast(I32)

    def words4(ap):
        return ap[0].bitcast(I32)

    def scale_rows(ap):
        return ap[0].bitcast(I32).rearrange("(q r) n -> r q n", q=QUADS)

    with ExitStack() as ctx:
        sb = ctx.enter_context(tc.tile_pool(name="sb", bufs=1))
        ps = ctx.enter_context(tc.psum_pool(name="ps", bufs=1))

        def tile(name, shape, dtype, tag=None):
            return sb.tile(shape, dtype, name=name, tag=tag or name, align_bytes=64)

        o1 = tile("o1", [P, J // 16], U16)
        o2 = tile("o2", [P, J // 16], U16)
        o3 = tile("o3", [P, J // 16], U16)
        o4 = tile("o4", [P, O // 16], U16)
        o5 = tile("o5", [P, O // 16], U16)
        o6 = tile("o6", [P, O // 16], U16)
        o7 = tile("o7", [P, O // 16], U16)
        gs_sb = tile("gs_sb", [P, PACK], F32)
        cq_sb = [tile("cq%d" % t, [P, T], F32) for t in range(PACK)]
        xo_w = tile("xo_w", [P, Z], I32)
        w_raw = tile("w_raw", [P, R], I32)
        w2_raw = tile("w2_raw", [P, R // 2], I32)
        wb_w = tile("wb_w", [P, 2 * N], U8)
        ws_w = tile("ws_w", [P, N], I32)
        sx_w = tile("sx_w", [P, O], I32)
        stage_x = tile("stage_x", [16, Z // 4], I32)
        stage_a = tile("stage_a", [8, QUADS, R // 4], I32)
        plane_b = tile("plane_b", [P, N], U8)
        plane_x = tile("plane_x", [P, Z], U8)
        raw_a = tile("raw_a", [P, 2, R // 4], I32)
        plane_a = tile("plane_a", [P, R], U8)
        xg_s = tile("xg_s", [P, J], U8)
        pw = [tile("pw%d" % t, [P, C], F32) for t in range(PACK)]
        pa = [tile("pa%d" % h, [P, E], F32) for h in range(2)]
        pb = [tile("pb%d" % h, [P, E], F32) for h in range(2)]

        nc.vector.memset(plane_x[:].bitcast(I32), 0)
        nc.vector.memset(raw_a[:], 0)
        nc.vector.memset(xg_s[:].bitcast(I32), 0)
        nc.vector.memset(plane_b[:].bitcast(I32), 0)

        cq_rows = cq.rearrange("(p t) n -> p t n", t=PACK)
        nc.sync.dma_start(stage_a[4:8], scale_rows(w_scales))
        nc.sync.dma_start(stage_a[0:4], scale_rows(w2_scales))
        nc.sync.dma_start(stage_x[:], xo_scales[0].bitcast(I32))
        nc.sync.dma_start(cq_sb[0][:], cq_rows[:, 0, :])
        nc.sync.dma_start(o1[:], offs)
        nc.sync.dma_start(gs_sb[:], gs.rearrange("(p t) o -> p (t o)", t=PACK))
        nc.sync.dma_start(o2[:], offs2)
        for t in range(1, PACK):
            nc.sync.dma_start(cq_sb[t][:], cq_rows[:, t, :])
        nc.sync.dma_start(w_raw[:], words8(w_words))
        nc.sync.dma_start(w2_raw[:], words4(w2_words))
        nc.sync.dma_start(xo_w[:], words8(xo_words))

        nc.vector.tensor_copy(plane_x[:].bitcast(I32)[0:16, :], stage_x[:])
        xg_rows = tile("xg_rows", [P, J], U8)
        nc.vector.tensor_copy(xg_rows[:], plane_x[:].indirect(o2[:]))
        nc.vector.tensor_copy(xg_s[:].bitcast(I32)[0:4, :], xg_rows[:].bitcast(I32)[0:4, :])
        for q in range(1, QUADS):
            nc.sync.dma_start(xg_s[:].bitcast(I32)[32 * q : 32 * q + 4, :], xg_rows[:].bitcast(I32)[4 * q : 4 * q + 4, :])

        nc.sync.dma_start(o3[:], offs3)
        nc.sync.dma_start(o5[:], offs5)
        nc.sync.dma_start(o4[:], offs4)
        nc.sync.dma_start(o7[:], offs7)
        nc.sync.dma_start(o6[:], offs6)
        nc.sync.dma_start(sx_w[:], words8(sx_words))
        nc.sync.dma_start(ws_w[:], words8(ws_words))
        nc.sync.dma_start(wb_w[:].bitcast(I32), words4(wb_words))
        for first, scales, width in ((4, sx_scales, O), (8, ws_scales, N), (0, wb_scales, N)):
            for q in range(QUADS):
                nc.sync.dma_start(
                    plane_b[32 * q + first : 32 * q + first + 4, 0:width].bitcast(I32),
                    scales[0].bitcast(I32)[4 * q : 4 * q + 4, :],
                )


        for q in (2, 3, 0, 1):
            nc.vector.tensor_copy(raw_a[32 * (q % 2) : 32 * (q % 2) + 8, q // 2, :], stage_a[:, q, :])
        nc.vector.tensor_copy(raw_a[64:P, 0, :], raw_a[0:64, 1, :])
        nc.vector.tensor_copy(
            plane_a[:].rearrange("p (t m) -> p m t", t=PACK),
            raw_a[:, 0, :].bitcast(U8).rearrange("p (m t) -> p m t", t=PACK),
        )
        for page in pw + pa + pb:
            nc.vector.memset(page[:].bitcast(I32), 0)

        x1_pairs = [tile("x1_pair%d" % u, [P, 2, J], BF16) for u in range(2)]
        x1_in = tile("x1_in", [P, J, PACK], BF16)
        for t in range(PACK):
            nc.scalar.activation(
                x1_pairs[t // 2][:, t % 2, :], cq_sb[t][:].indirect(o1[:]), COPY, scale=gs_sb[:, t : t + 1]
            )
            if t % 2 == 1:
                nc.vector.tensor_copy(x1_in[:, :, t - 1 : t + 1], x1_pairs[t // 2][:].rearrange("p t j -> p j t"))
        x1_w = tile("x1_w", [P, J], U32)
        x1_s = tile("x1_s", [P, J], U8)
        nc.vector.quantize_mx(out=x1_w[:].bitcast(E4M3), scales=x1_s[:], in_=x1_in[:].rearrange("p j t -> p (j t)"))

        w_w = tile("w_w", [P, R], U32)
        nc.scalar.copy(
            w_w[:].rearrange("p (t m) -> p m t", t=PACK),
            w_raw[:].bitcast(U32).rearrange("p (m t) -> p m t", t=PACK),
        )
        w2_w = tile("w2_w", [P, 2 * R], U8)
        nc.scalar.copy(
            w2_w[:].bitcast(U16).rearrange("p (t m) -> p m t", t=PACK),
            w2_raw[:].bitcast(U16).rearrange("p (m t) -> p m t", t=PACK),
        )
        xg_w = tile("xg_w", [P, J], U32)
        nc.vector.tensor_copy(xg_w[:], xo_w[:].bitcast(U32).indirect(o2[:]))

        a_lone = [ps.tile([P, J], F32, name="a_ps%d" % t) for t in range(2)]
        a_pair = ps.tile([P, 2, J], F32, name="a_pair")
        a_ps = [a_lone[0][:], a_lone[1][:], a_pair[:, 0, :], a_pair[:, 1, :]]
        b_ps = [ps.tile([P, 2, J], F32, name="b_ps%d" % u) for u in range(2)]
        p_ps = [ps.tile([P, O], F32, name="p_ps%d" % h) for h in range(2)]
        for t in range(PACK):
            cols = slice(P * t, P * (t + 1))
            nc.tensor.matmul_mx(
                out=a_ps[t], lhsT=w_w[:, cols].bitcast(E4M3), lhsT_scale=plane_a[4:P, cols],
                rhs=x1_w[:].bitcast(E4M3), rhs_scale=x1_s[:], start=True, stop=True,
            )
        for t in range(PACK):
            cols = slice(P * t, P * (t + 1))
            nc.tensor.matmul_mx(
                out=b_ps[t // 2][:, t % 2, :], lhsT=w2_w[:, 2 * P * t : 2 * P * (t + 1)].bitcast(E2M1),
                lhsT_scale=plane_a[:, cols], rhs=xg_w[:].bitcast(E4M3), rhs_scale=xg_s[:], start=True, stop=True,
            )

        a_first = tile("a_first", [P, J], F32, tag="w2_raw")
        a_rest = tile("a_rest", [P, PACK - 1, J], F32, tag="xo_w")
        a_sb = [a_first[:]] + [a_rest[:, t, :] for t in range(PACK - 1)]
        b_sb = [tile("b_sb%d" % t, [P, J], F32) for t in range(PACK)]
        from_pw = [tile("from_pw%d" % u, [P, 2, O], F32) for u in range(2)]
        from_b = [tile("from_b%d" % u, [P, 2, O], F32) for u in range(2)]

        def gather_pw(t):
            nc.scalar.activation(from_pw[t // 2][:, t % 2, :], pw[t][:].indirect(o4[:]), COPY, scale=b_sb[t][:, 0:1])

        nc.scalar.copy(a_sb[0], a_ps[0])
        nc.scalar.activation(pw[0][:].indirect(o3[:]), a_sb[0], COPY)
        nc.vector.tensor_copy(a_sb[1], a_ps[1])
        nc.vector.tensor_copy(a_rest[:, 1:3, :], a_pair[:])
        for t in range(1, PACK):
            nc.vector.tensor_copy(pw[t][:].indirect(o3[:]), a_sb[t])
        for t in range(PACK):
            nc.scalar.copy(b_sb[t][:], b_ps[t // 2][:, t % 2, :])
        for t in range(PACK):
            nc.scalar.activation(from_b[t // 2][:, t % 2, :], b_sb[t][:].indirect(o5[:]), COPY, scale=a_sb[t][:, 0:1])
        for t in range(PACK):
            gather_pw(t)

        for h in range(2):
            cols = slice(P * h, P * (h + 1))
            nc.tensor.matmul_mx(
                out=p_ps[h][:], lhsT=ws_w[:, cols].bitcast(E4M3), lhsT_scale=plane_b[8:P, cols],
                rhs=sx_w[:].bitcast(E4M3), rhs_scale=plane_b[4:P, 0:O], start=True, stop=False,
            )

        hid_in = tile("hid_in", [P, O, PACK], BF16, tag="xo_w")
        for u in range(2):
            nc.vector.tensor_max(
                hid_in[:, :, 2 * u : 2 * u + 2].rearrange("p (c i) t -> p c t i", i=4),
                from_pw[u][:].rearrange("p t (c i) -> p c t i", i=4),
                from_b[u][:].rearrange("p t (c i) -> p c t i", i=4),
            )
        hid_w = tile("hid_w", [P, O], U32)
        hid_s = tile("hid_s", [P, O], U8)
        nc.vector.quantize_mx(out=hid_w[:].bitcast(E5M2), scales=hid_s[:], in_=hid_in[:].rearrange("p o t -> p (o t)"))
        for h in range(2):
            nc.tensor.matmul_mx(
                out=p_ps[h][:], lhsT=wb_w[:, 2 * P * h : 2 * P * (h + 1)].bitcast(E2M1),
                lhsT_scale=plane_b[:, P * h : P * (h + 1)], rhs=hid_w[:].bitcast(E5M2), rhs_scale=hid_s[:],
                start=False, stop=True,
            )

        p_sb = [tile("p_sb%d" % h, [P, O], F32) for h in range(2)]
        y = [tile("y%d" % h, [P, E], F32) for h in range(2)]
        nc.scalar.copy(p_sb[0][:], p_ps[0][:])
        nc.vector.tensor_copy(p_sb[1][:], p_ps[1][:])
        half = O // 2
        nc.scalar.activation(pb[0][:].indirect(o7[:]), p_sb[0][:], COPY)
        nc.vector.tensor_copy(pa[1][:].indirect(o6[:, 0 : half // 16]), p_sb[1][:, 0:half])
        nc.vector.tensor_copy(pa[0][:].indirect(o6[:]), p_sb[0][:])
        nc.scalar.activation(pb[1][:].indirect(o7[:]), p_sb[1][:], COPY)
        nc.scalar.activation(pa[1][:].indirect(o6[:, half // 16 : O // 16]), p_sb[1][:, half:O], COPY)
        for h in range(2):
            pieces = 1 + h
            for piece in range(pieces):
                cols = slice(E // pieces * piece, E // pieces * (piece + 1))
                nc.vector.tensor_add(y[h][:, cols], pa[h][:, cols], pb[h][:, cols])
                nc.sync.dma_start(out[P * h : P * (h + 1), cols], y[h][:, cols])
